import numpy as np
import ml_dtypes


def mxq(x, axis, fmt="e4m3"):
    dtype, down = {"e4m3": (ml_dtypes.float8_e4m3fn, 7), "e5m2": (ml_dtypes.float8_e5m2, 14)}[fmt]
    v = np.moveaxis(np.asarray(x, np.float32).astype(ml_dtypes.bfloat16).astype(np.float64), axis, -1)
    blocks = v.reshape(v.shape[:-1] + (-1, 32))
    amax = np.abs(blocks).max(-1, keepdims=True)
    byte = np.maximum(np.where(amax > 0, np.frexp(amax)[1] - 1 + 127, 0) - down, 1)
    scale = np.exp2(byte - 127.0)
    codes = (blocks / scale).astype(np.float32).astype(dtype).astype(np.float64)
    return np.moveaxis((codes * scale).reshape(v.shape), -1, axis)


WIDE = False


def mx_kscale(k):
    if not WIDE:
        return np.ones(k)
    levels = np.array([30, -30])
    if k % 512:
        return np.exp2(np.random.permutation(np.resize(levels, k // 32))).repeat(32)
    a = np.empty((k // 512, 16))
    for p in range(k // 512):
        a[p, :8] = np.random.permutation(np.resize(levels, 8))
        for g in range(8):
            far = levels[np.abs(levels - a[p, g]) >= 10]
            a[p, g + 8] = far[np.random.randint(len(far))]
    return np.exp2(a.ravel()).repeat(32)


def f64(x):
    return np.asarray(x).astype(np.float64)


E2M1 = np.array([0.0, 0.5, 1.0, 1.5, 2.0, 3.0, 4.0, 6.0, -0.0, -0.5, -1.0, -1.5, -2.0, -3.0, -4.0, -6.0])


def pack_weight(w, fmt):
    k, n = w.shape
    w = f64(np.asarray(w, np.float32).astype(ml_dtypes.bfloat16)).reshape(k // 32, 32, n)
    amax = np.abs(w).max(1)
    if fmt == "e4m3":
        byte = np.frexp(amax)[1] - 1 + 127 - 7
    else:
        mant, ex = np.frexp(amax / 6.0)
        byte = np.where(mant > 0.5, ex, ex - 1) + 127
    byte = np.clip(np.where(amax > 0, byte, 1), 1, 254)
    scaled = (w * np.exp2(127.0 - byte)[:, None, :]).reshape(k, n).astype(np.float32)
    by_word = np.ascontiguousarray(scaled.reshape(k // 512, 128, 4, n).transpose(0, 1, 3, 2))
    if fmt == "e4m3":
        words = by_word.astype(ml_dtypes.float8_e4m3fn).view(np.uint8)
    else:
        c = by_word.astype(ml_dtypes.float4_e2m1fn).view(np.uint8) & 0xF
        words = (c[..., 0::2] | (c[..., 1::2] << 4)).reshape(k // 512, 128, 2 * n)
    return np.ascontiguousarray(words), np.ascontiguousarray(byte.astype(np.uint8).reshape(k // 512, 16, n))


def unpack_weight(words, scales, fmt):
    g, _, n = scales.shape
    words = np.ascontiguousarray(words).reshape(g, 128, n, -1)
    if fmt == "e4m3":
        vals = words.view(ml_dtypes.float8_e4m3fn).astype(np.float64)
    else:
        nib = np.empty((g, 128, n, 4), np.uint8)
        nib[..., 0::2] = words & 0xF
        nib[..., 1::2] = words >> 4
        vals = E2M1[nib]
    vals = vals * np.repeat(np.exp2(scales.astype(np.float64) - 127.0), 8, axis=1)[..., None]
    return vals.transpose(0, 1, 3, 2).reshape(g * 512, n)


K, T, N = 1024, 512, 512


def setup_inputs():
    n = np.random.standard_normal
    fk = mx_kscale(K)
    wap = pack_weight(n((K, N)) * 1 / np.sqrt(K) * fk[:, None], "e2m1")
    wbp = pack_weight(n((K, N)) * 1 / np.sqrt(K) * fk[:, None], "e4m3")
    return {
        "xf": (n((K, T))).astype(np.float32),
        "fa": (np.random.uniform(0.5, 2.0, (K, 1)) / fk[:, None]).astype(np.float32),
        "fb": (np.random.uniform(0.5, 2.0, (K, 1)) / fk[:, None]).astype(np.float32),
        "wa_words": wap[0],
        "wa_scales": wap[1],
        "wb_words": wbp[0],
        "wb_scales": wbp[1],
    }


def reference(xf, fa, fb, wa_words, wa_scales, wb_words, wb_scales):
    wau = unpack_weight(wa_words, wa_scales, "e2m1")
    wbu = unpack_weight(wb_words, wb_scales, "e4m3")
    x1 = np.pad(f64(xf), ((0, 0), (1, 0)))[:, :T]
    x2 = np.pad(f64(xf), ((0, 0), (2, 0)))[:, :T]
    m = np.maximum(x1, x2)
    ua = np.maximum(f64(xf) - m, 0.0) * f64(fa)
    ub = np.maximum(m - f64(xf), 0.0) * f64(fb)
    uaq = mxq(ua, 0, "e5m2")
    ubq = mxq(ub, 0, "e4m3")
    y = wau.T @ uaq + wbu.T @ ubq
    return y

@@ -1,0 +1,239 @@
+from contextlib import ExitStack
+
+import concourse.mybir as mybir
+
+K, T, N = 1024, 512, 512
+FLOPS = 2 * 2 * K * T * N
+
+F32 = mybir.dt.float32
+BF16 = mybir.dt.bfloat16
+I32 = mybir.dt.int32
+U32 = mybir.dt.uint32
+U8 = mybir.dt.uint8
+E2M1X4 = mybir.dt.float4_e2m1fn_x4
+E4M3X4 = mybir.dt.float8_e4m3fn_x4
+E5M2X4 = mybir.dt.float8_e5m2_x4
+ALU = mybir.AluOpType
+ACT = mybir.ActivationFunctionType
+
+P = 128
+PACK = 4
+K_PASS = P * PACK
+PASSES = K // K_PASS
+N_TILES = N // P
+BANK = 512
+HALF = T // 2
+LEAD = 8
+RANGES = ((0, 256), (256, 384), (384, 512))
+PAD = BANK - RANGES[0][1]
+RUN = 4
+
+
+def tile_mix_ahead_and_behind_kernel(tc, xf, fa, fb, wa_words, wa_scales, wb_words, wb_scales, out):
+    nc = tc.nc
+    units = [(t0, t1, g) for t0, t1 in RANGES for g in range(PASSES)]
+    last = len(units) - 1
+
+    with ExitStack() as ctx:
+        keep = ctx.enter_context(tc.tile_pool(name="keep", bufs=1))
+        work = ctx.enter_context(tc.tile_pool(name="work", bufs=len(units)))
+        psum = ctx.enter_context(tc.psum_pool(name="psum", bufs=2))
+        ctx.enter_context(tc.manual_schedule())
+
+        x = {(h, g): keep.tile([P, PACK, LEAD + HALF], F32, name="x%d%d" % (h, g)) for h in range(2) for g in range(PASSES)}
+        fa_sb = keep.tile([P, PASSES, PACK], F32)
+        fb_sb = keep.tile([P, PASSES, PACK], F32)
+        fb_neg = keep.tile([P, PASSES, PACK], F32)
+        zeros = keep.tile([P, PACK, LEAD], F32)
+        wa_sb = keep.tile([P, PASSES, 2 * N], U8, align_bytes=64)
+        wb_sb = keep.tile([P, PASSES, N], U32, align_bytes=64)
+        wa_sc = keep.tile([P, PASSES, N], U8, align_bytes=64)
+        wb_sc = keep.tile([P, PASSES, N], U8, align_bytes=64)
+        ua_codes = [keep.tile([P, PAD + T], U32, align_bytes=64, name="ua_codes%d" % g) for g in range(PASSES)]
+        ua_sc = [keep.tile([P, PAD + T], U8, align_bytes=64, name="ua_sc%d" % g) for g in range(PASSES)]
+        ub_codes = [keep.tile([P, T], U32, align_bytes=64, name="ub_codes%d" % g) for g in range(PASSES)]
+        ub_sc = [keep.tile([P, T], U8, align_bytes=64, name="ub_sc%d" % g) for g in range(PASSES)]
+
+        nc.vector.memset(zeros[:], 0.0)
+        nc.vector.memset(wa_sc[:].bitcast(U32), 0)
+        nc.vector.memset(wb_sc[:].bitcast(U32), 0)
+        for g in range(PASSES):
+            nc.vector.memset(ua_codes[g][:, :PAD], 0)
+            nc.vector.memset(ua_sc[g][:, :PAD].bitcast(U32), 0)
+
+        def load_x(h, g, js):
+            lo = max(h * HALF - 2, 0)
+            hi = (h + 1) * HALF
+            rows = xf[g * K_PASS : (g + 1) * K_PASS, lo:hi].rearrange("(p j) t -> p j t", j=PACK)
+            nc.sync.dma_start(out=x[h, g][:, js, LEAD + HALF - (hi - lo) :], in_=rows[:, js, :])
+
+        def load_scales(plane, scales):
+            for q in range(4):
+                nc.sync.dma_start(
+                    out=plane[32 * q : 32 * q + 4, :, :].bitcast(I32),
+                    in_=scales[:, 4 * q : 4 * q + 4, :].rearrange("g r c -> r g c").bitcast(I32),
+                )
+
+        every_j = slice(0, PACK)
+        j_halves = (slice(0, 2), slice(2, 4))
+        j_first = (slice(0, 1), slice(1, 2), slice(2, 4))
+        for js in j_first:
+            load_x(0, 0, js)
+        nc.sync.dma_start(out=fa_sb[:], in_=fa.rearrange("(g p j) o -> p g (j o)", g=PASSES, j=PACK))
+        nc.sync.dma_start(out=fb_sb[:], in_=fb.rearrange("(g p j) o -> p g (j o)", g=PASSES, j=PACK))
+        load_x(0, 1, every_j)
+        load_x(1, 0, every_j)
+        nc.sync.dma_start(out=wa_sb[:].bitcast(I32), in_=wa_words.rearrange("g p c -> p g c").bitcast(I32))
+        nc.sync.dma_start(out=wb_sb[:].bitcast(I32), in_=wb_words.rearrange("g p c r -> p g (c r)").bitcast(I32))
+        load_scales(wa_sc, wa_scales)
+        load_scales(wb_sc, wb_scales)
+        load_x(1, 1, every_j)
+
+        for g in range(PASSES):
+            nc.scalar.copy(out=x[0, g][:, :, :LEAD], in_=zeros[:])
+
+        short, peak, diff, rows_a, rows_b, grouped_a, grouped_b, acc = {}, {}, {}, {}, {}, {}, {}, {}
+
+        def shifted(u, js, back):
+            t0, t1, g = units[u]
+            h = t0 // HALF
+            c0 = LEAD + t0 - h * HALF - back
+            return x[h, g][:, js, c0 : c0 + t1 - t0]
+
+        def width(u):
+            return units[u][1] - units[u][0]
+
+        def find_peak(u, js):
+            if u not in peak:
+                peak[u] = work.tile([P, PACK, width(u)], F32, name="peak")
+            nc.vector.tensor_tensor(out=peak[u][:, js, :], in0=shifted(u, js, 1), in1=shifted(u, js, 2), op=ALU.max)
+
+        def subtract_peak(u, js):
+            if u not in diff:
+                diff[u] = work.tile([P, PACK, width(u)], F32, name="diff")
+            nc.vector.tensor_tensor(out=diff[u][:, js, :], in0=shifted(u, js, 0), in1=peak[u][:, js, :], op=ALU.subtract)
+
+        def scale_a(u, js):
+            g = units[u][2]
+            if u not in rows_a:
+                rows_a[u] = work.tile([P, PACK, width(u)], BF16, name="rows_a")
+            for j in js:
+                nc.vector.tensor_scalar(
+                    out=rows_a[u][:, j, :], in0=diff[u][:, j, :], scalar1=0.0, scalar2=fa_sb[:, g, j : j + 1], op0=ALU.max, op1=ALU.mult
+                )
+
+        def scale_b(u):
+            g = units[u][2]
+            rows_b[u] = work.tile([P, PACK, width(u)], BF16, name="rows_b")
+            for j in range(PACK):
+                nc.vector.tensor_scalar(
+                    out=rows_b[u][:, j, :], in0=diff[u][:, j, :], scalar1=0.0, scalar2=fb_neg[:, g, j : j + 1], op0=ALU.min, op1=ALU.mult
+                )
+
+        def clip_b(u, js):
+            if u not in short:
+                short[u] = work.tile([P, PACK, width(u)], F32, name="short")
+            nc.scalar.activation(out=short[u][:, js, :], in_=diff[u][:, js, :], func=ACT.Relu, scale=-1.0)
+
+        def scale_b_scalar(u):
+            g = units[u][2]
+            rows_b[u] = work.tile([P, PACK, width(u)], BF16, name="rows_b")
+            for j in range(PACK):
+                nc.scalar.activation(out=rows_b[u][:, j, :], in_=short[u][:, j, :], func=ACT.Copy, scale=fb_sb[:, g, j : j + 1])
+
+        def interleave(copy, rows, name):
+            grouped = work.tile([P, rows.shape[2], PACK], BF16, align_bytes=64, name=name)
+            copy(
+                out=grouped[:].rearrange("p (c i) j -> p c j i", i=RUN),
+                in_=rows[:].rearrange("p j (c i) -> p c j i", i=RUN),
+            )
+            return grouped
+
+        def quantize_a(u):
+            t0, t1, g = units[u]
+            cols = slice(PAD + t0, PAD + t1)
+            nc.vector.quantize_mx(
+                out=ua_codes[g][:, cols].bitcast(E5M2X4), scales=ua_sc[g][:, cols], in_=grouped_a[u][:].rearrange("p t j -> p (t j)")
+            )
+
+        def quantize_b(u):
+            t0, t1, g = units[u]
+            nc.vector.quantize_mx(
+                out=ub_codes[g][:, t0:t1].bitcast(E4M3X4), scales=ub_sc[g][:, t0:t1], in_=grouped_b[u][:].rearrange("p t j -> p (t j)")
+            )
+
+        def multiply_a(u):
+            t0, t1, g = units[u]
+            cols = slice(PAD + t1 - BANK, PAD + t1)
+            for n in range(N_TILES):
+                if g == 0:
+                    acc[t0, n] = psum.tile([P, BANK], F32, name="acc%d" % n)
+                nc.tensor.matmul_mx(
+                    out=acc[t0, n][:],
+                    lhsT=wa_sb[:, g, 2 * P * n : 2 * P * (n + 1)].bitcast(E2M1X4),
+                    lhsT_scale=wa_sc[:, g, P * n : P * (n + 1)],
+                    rhs=ua_codes[g][:, cols].bitcast(E5M2X4),
+                    rhs_scale=ua_sc[g][:, cols],
+                    start=(g == 0),
+                    stop=False,
+                )
+
+        def multiply_b(u):
+            t0, t1, g = units[u]
+            for n in range(N_TILES):
+                nc.tensor.matmul_mx(
+                    out=acc[t0, n][:, BANK - (t1 - t0) :],
+                    lhsT=wb_sb[:, g, P * n : P * (n + 1)].bitcast(E4M3X4),
+                    lhsT_scale=wb_sc[:, g, P * n : P * (n + 1)],
+                    rhs=ub_codes[g][:, t0:t1].bitcast(E4M3X4),
+                    rhs_scale=ub_sc[g][:, t0:t1],
+                    start=False,
+                    stop=(g == PASSES - 1),
+                )
+
+        def store(u, n, copy):
+            t0, t1, g = units[u]
+            result = work.tile([P, t1 - t0], F32, name="result%d" % n)
+            copy(out=result[:], in_=acc[t0, n][:, BANK - (t1 - t0) :])
+            nc.sync.dma_start(out=out[P * n : P * (n + 1), t0:t1], in_=result[:])
+
+        find_peak(0, j_first[0])
+        find_peak(0, j_first[1])
+        subtract_peak(0, j_halves[0])
+        clip_b(0, j_halves[0])
+        find_peak(0, j_halves[1])
+        scale_a(0, (0, 1))
+        subtract_peak(0, j_halves[1])
+        clip_b(0, j_halves[1])
+        nc.scalar.activation(out=fb_neg[:], in_=fb_sb[:], func=ACT.Copy, scale=-1.0)
+
+        for u in range(len(units)):
+            if u == 0:
+                find_peak(1, every_j)
+                scale_a(0, (2, 3))
+            else:
+                scale_a(u, range(PACK))
+            grouped_a[u] = interleave(nc.scalar.copy, rows_a[u], "grouped_a")
+            if 0 < u < last:
+                find_peak(u + 1, every_j)
+            if u > 0:
+                quantize_b(u - 1)
+                multiply_b(u - 1)
+            if u == 0:
+                scale_b_scalar(u)
+            else:
+                scale_b(u)
+            if u < last:
+                grouped_b[u] = interleave(nc.scalar.copy, rows_b[u], "grouped_b")
+                subtract_peak(u + 1, every_j)
+            if u >= PASSES and u % PASSES == 0:
+                for n in range(N_TILES):
+                    store(u - 1, n, nc.scalar.copy)
+            quantize_a(u)
+            multiply_a(u)
+
+        grouped_b[last] = interleave(nc.vector.tensor_copy, rows_b[last], "grouped_b")
+        quantize_b(last)
+        multiply_b(last)
+        for n in range(N_TILES):
+            store(last, n, nc.scalar.copy if n % 2 == 0 else nc.vector.tensor_copy)

@@ -25,8 +25,10 @@ BANK = 512
 HALF = T // 2
 LEAD = 8
 RANGES = ((0, 256), (256, 384), (384, 512))
+XS = ((0, 256), (256, 512))
 PAD = BANK - RANGES[0][1]
 RUN = 4
+ORDER = "Ng0 A_00 A_01 B_00 B_01 A_023 Ca001 B_023 Cb001 Ca023 Ia0 A_1 Cb023 Ib0 B_1 Qa0 Ca1 Ia1 A_2 Qb0 Cb1 Ib1 B_2 Qa1 Ca2 Ia2 A_3 Qb1 Cb2 Ib2 B_3 St10S St11S St12S St13S Qa2 Ca3 Ia3 A_4 Qb2 Cb3 Ib3 B_4 Qa3 Ca4 Ia4 A_5 Qb3 Cb4 Ib4 B_5 Qa4 St30S St31S St32S St33S Ca5 Qb4 Ia5V Cb5 Ib5 Qa5 Qb5 St50V St51S St52V St53S"
 
 
 def tile_mix_ahead_and_behind_kernel(tc, xf, fa, fb, wa_words, wa_scales, wb_words, wb_scales, out):
@@ -40,7 +42,7 @@ def tile_mix_ahead_and_behind_kernel(tc, xf, fa, fb, wa_words, wa_scales, wb_wor
         psum = ctx.enter_context(tc.psum_pool(name="psum", bufs=2))
         ctx.enter_context(tc.manual_schedule())
 
-        x = {(h, g): keep.tile([P, PACK, LEAD + HALF], F32, name="x%d%d" % (h, g)) for h in range(2) for g in range(PASSES)}
+        x = {(h, g): keep.tile([P, PACK, LEAD + XS[h][1] - XS[h][0]], F32, name="x%d%d" % (h, g)) for h in range(2) for g in range(PASSES)}
         fa_sb = keep.tile([P, PASSES, PACK], F32)
         fb_sb = keep.tile([P, PASSES, PACK], F32)
         fb_neg = keep.tile([P, PASSES, PACK], F32)
@@ -55,6 +57,7 @@ def tile_mix_ahead_and_behind_kernel(tc, xf, fa, fb, wa_words, wa_scales, wb_wor
         ub_sc = [keep.tile([P, T], U8, align_bytes=64, name="ub_sc%d" % g) for g in range(PASSES)]
 
         nc.vector.memset(zeros[:], 0.0)
+        nc.vector.memset(x[0, 0][:, :, :LEAD], 0.0)
         nc.vector.memset(wa_sc[:].bitcast(U32), 0)
         nc.vector.memset(wb_sc[:].bitcast(U32), 0)
         for g in range(PASSES):
@@ -62,10 +65,10 @@ def tile_mix_ahead_and_behind_kernel(tc, xf, fa, fb, wa_words, wa_scales, wb_wor
             nc.vector.memset(ua_sc[g][:, :PAD].bitcast(U32), 0)
 
         def load_x(h, g, js):
-            lo = max(h * HALF - 2, 0)
-            hi = (h + 1) * HALF
+            lo = max(XS[h][0] - 2, 0)
+            hi = XS[h][1]
             rows = xf[g * K_PASS : (g + 1) * K_PASS, lo:hi].rearrange("(p j) t -> p j t", j=PACK)
-            nc.sync.dma_start(out=x[h, g][:, js, LEAD + HALF - (hi - lo) :], in_=rows[:, js, :])
+            nc.sync.dma_start(out=x[h, g][:, js, LEAD + lo - XS[h][0] :], in_=rows[:, js, :])
 
         def load_scales(plane, scales):
             for q in range(4):
@@ -77,10 +80,11 @@ def tile_mix_ahead_and_behind_kernel(tc, xf, fa, fb, wa_words, wa_scales, wb_wor
         every_j = slice(0, PACK)
         j_halves = (slice(0, 2), slice(2, 4))
         j_first = (slice(0, 1), slice(1, 2), slice(2, 4))
-        for js in j_first:
+        for js in j_first[:2]:
             load_x(0, 0, js)
         nc.sync.dma_start(out=fa_sb[:], in_=fa.rearrange("(g p j) o -> p g (j o)", g=PASSES, j=PACK))
         nc.sync.dma_start(out=fb_sb[:], in_=fb.rearrange("(g p j) o -> p g (j o)", g=PASSES, j=PACK))
+        load_x(0, 0, j_first[2])
         load_x(0, 1, every_j)
         load_x(1, 0, every_j)
         nc.sync.dma_start(out=wa_sb[:].bitcast(I32), in_=wa_words.rearrange("g p c -> p g c").bitcast(I32))
@@ -89,16 +93,18 @@ def tile_mix_ahead_and_behind_kernel(tc, xf, fa, fb, wa_words, wa_scales, wb_wor
         load_scales(wb_sc, wb_scales)
         load_x(1, 1, every_j)
 
-        for g in range(PASSES):
-            nc.scalar.copy(out=x[0, g][:, :, :LEAD], in_=zeros[:])
+        nc.scalar.copy(out=x[0, 1][:, :, :LEAD], in_=zeros[:])
 
         short, peak, diff, rows_a, rows_b, grouped_a, grouped_b, acc = {}, {}, {}, {}, {}, {}, {}, {}
 
         def shifted(u, js, back):
             t0, t1, g = units[u]
-            h = t0 // HALF
-            c0 = LEAD + t0 - h * HALF - back
+            h = 0 if t0 < XS[0][1] else 1
+            c0 = LEAD + t0 - XS[h][0] - back
             return x[h, g][:, js, c0 : c0 + t1 - t0]
+
+        def pieces(w):
+            return ((0, 256), (256, 384)) if w == 384 else ((0, w),)
 
         def width(u):
             return units[u][1] - units[u][0]
@@ -122,10 +128,11 @@ def tile_mix_ahead_and_behind_kernel(tc, xf, fa, fb, wa_words, wa_scales, wb_wor
                     out=rows_a[u][:, j, :], in0=diff[u][:, j, :], scalar1=0.0, scalar2=fa_sb[:, g, j : j + 1], op0=ALU.max, op1=ALU.mult
                 )
 
-        def scale_b(u):
+        def scale_b(u, js):
             g = units[u][2]
-            rows_b[u] = work.tile([P, PACK, width(u)], BF16, name="rows_b")
-            for j in range(PACK):
+            if u not in rows_b:
+                rows_b[u] = work.tile([P, PACK, width(u)], BF16, name="rows_b")
+            for j in js:
                 nc.vector.tensor_scalar(
                     out=rows_b[u][:, j, :], in0=diff[u][:, j, :], scalar1=0.0, scalar2=fb_neg[:, g, j : j + 1], op0=ALU.min, op1=ALU.mult
                 )
@@ -135,10 +142,11 @@ def tile_mix_ahead_and_behind_kernel(tc, xf, fa, fb, wa_words, wa_scales, wb_wor
                 short[u] = work.tile([P, PACK, width(u)], F32, name="short")
             nc.scalar.activation(out=short[u][:, js, :], in_=diff[u][:, js, :], func=ACT.Relu, scale=-1.0)
 
-        def scale_b_scalar(u):
+        def scale_b_scalar(u, js):
             g = units[u][2]
-            rows_b[u] = work.tile([P, PACK, width(u)], BF16, name="rows_b")
-            for j in range(PACK):
+            if u not in rows_b:
+                rows_b[u] = work.tile([P, PACK, width(u)], BF16, name="rows_b")
+            for j in js:
                 nc.scalar.activation(out=rows_b[u][:, j, :], in_=short[u][:, j, :], func=ACT.Copy, scale=fb_sb[:, g, j : j + 1])
 
         def interleave(copy, rows, name):
@@ -151,16 +159,19 @@ def tile_mix_ahead_and_behind_kernel(tc, xf, fa, fb, wa_words, wa_scales, wb_wor
 
         def quantize_a(u):
             t0, t1, g = units[u]
-            cols = slice(PAD + t0, PAD + t1)
-            nc.vector.quantize_mx(
-                out=ua_codes[g][:, cols].bitcast(E5M2X4), scales=ua_sc[g][:, cols], in_=grouped_a[u][:].rearrange("p t j -> p (t j)")
-            )
+            for c0, c1 in pieces(t1 - t0):
+                cols = slice(PAD + t0 + c0, PAD + t0 + c1)
+                nc.vector.quantize_mx(
+                    out=ua_codes[g][:, cols].bitcast(E5M2X4), scales=ua_sc[g][:, cols], in_=grouped_a[u][:, c0:c1, :].rearrange("p t j -> p (t j)")
+                )
 
         def quantize_b(u):
             t0, t1, g = units[u]
-            nc.vector.quantize_mx(
-                out=ub_codes[g][:, t0:t1].bitcast(E4M3X4), scales=ub_sc[g][:, t0:t1], in_=grouped_b[u][:].rearrange("p t j -> p (t j)")
-            )
+            for c0, c1 in pieces(t1 - t0):
+                cols = slice(t0 + c0, t0 + c1)
+                nc.vector.quantize_mx(
+                    out=ub_codes[g][:, cols].bitcast(E4M3X4), scales=ub_sc[g][:, cols], in_=grouped_b[u][:, c0:c1, :].rearrange("p t j -> p (t j)")
+                )
 
         def multiply_a(u):
             t0, t1, g = units[u]
@@ -181,15 +192,16 @@ def tile_mix_ahead_and_behind_kernel(tc, xf, fa, fb, wa_words, wa_scales, wb_wor
         def multiply_b(u):
             t0, t1, g = units[u]
             for n in range(N_TILES):
-                nc.tensor.matmul_mx(
-                    out=acc[t0, n][:, BANK - (t1 - t0) :],
-                    lhsT=wb_sb[:, g, P * n : P * (n + 1)].bitcast(E4M3X4),
-                    lhsT_scale=wb_sc[:, g, P * n : P * (n + 1)],
-                    rhs=ub_codes[g][:, t0:t1].bitcast(E4M3X4),
-                    rhs_scale=ub_sc[g][:, t0:t1],
-                    start=False,
-                    stop=(g == PASSES - 1),
-                )
+                for c0, c1 in pieces(t1 - t0):
+                    nc.tensor.matmul_mx(
+                        out=acc[t0, n][:, BANK - (t1 - t0) + c0 : BANK - (t1 - t0) + c1],
+                        lhsT=wb_sb[:, g, P * n : P * (n + 1)].bitcast(E4M3X4),
+                        lhsT_scale=wb_sc[:, g, P * n : P * (n + 1)],
+                        rhs=ub_codes[g][:, t0 + c0 : t0 + c1].bitcast(E4M3X4),
+                        rhs_scale=ub_sc[g][:, t0 + c0 : t0 + c1],
+                        start=False,
+                        stop=(g == PASSES - 1 and c1 == t1 - t0),
+                    )
 
         def store(u, n, copy):
             t0, t1, g = units[u]
@@ -197,43 +209,35 @@ def tile_mix_ahead_and_behind_kernel(tc, xf, fa, fb, wa_words, wa_scales, wb_wor
             copy(out=result[:], in_=acc[t0, n][:, BANK - (t1 - t0) :])
             nc.sync.dma_start(out=out[P * n : P * (n + 1), t0:t1], in_=result[:])
 
-        find_peak(0, j_first[0])
-        find_peak(0, j_first[1])
-        subtract_peak(0, j_halves[0])
-        clip_b(0, j_halves[0])
-        find_peak(0, j_halves[1])
-        scale_a(0, (0, 1))
-        subtract_peak(0, j_halves[1])
-        clip_b(0, j_halves[1])
-        nc.scalar.activation(out=fb_neg[:], in_=fb_sb[:], func=ACT.Copy, scale=-1.0)
-
-        for u in range(len(units)):
-            if u == 0:
-                find_peak(1, every_j)
-                scale_a(0, (2, 3))
-            else:
-                scale_a(u, range(PACK))
-            grouped_a[u] = interleave(nc.scalar.copy, rows_a[u], "grouped_a")
-            if 0 < u < last:
-                find_peak(u + 1, every_j)
-            if u > 0:
-                quantize_b(u - 1)
-                multiply_b(u - 1)
-            if u == 0:
-                scale_b_scalar(u)
-            else:
-                scale_b(u)
-            if u < last:
-                grouped_b[u] = interleave(nc.scalar.copy, rows_b[u], "grouped_b")
-                subtract_peak(u + 1, every_j)
-            if u >= PASSES and u % PASSES == 0:
-                for n in range(N_TILES):
-                    store(u - 1, n, nc.scalar.copy)
-            quantize_a(u)
-            multiply_a(u)
-
-        grouped_b[last] = interleave(nc.vector.tensor_copy, rows_b[last], "grouped_b")
-        quantize_b(last)
-        multiply_b(last)
-        for n in range(N_TILES):
-            store(last, n, nc.scalar.copy if n % 2 == 0 else nc.vector.tensor_copy)
+        COPY = {"S": nc.scalar.copy, "V": nc.vector.tensor_copy}
+        for tok in ORDER.split():
+            op, u = tok[:2], int(tok[2])
+            rest = tok[3:]
+            js = [int(c) for c in rest if c in "0123"] or [0, 1, 2, 3]
+            sl = slice(js[0], js[-1] + 1)
+            if op == "A_":
+                find_peak(u, sl)
+            elif op == "B_":
+                subtract_peak(u, sl)
+            elif op == "Ca":
+                scale_a(u, js)
+            elif op == "Cb":
+                scale_b(u, js)
+            elif op == "Rb":
+                clip_b(u, sl)
+            elif op == "Zb":
+                scale_b_scalar(u, js)
+            elif op == "Ia":
+                grouped_a[u] = interleave(COPY[rest or "S"], rows_a[u], "grouped_a")
+            elif op == "Ib":
+                grouped_b[u] = interleave(COPY[rest or "S"], rows_b[u], "grouped_b")
+            elif op == "Qa":
+                quantize_a(u)
+                multiply_a(u)
+            elif op == "Qb":
+                quantize_b(u)
+                multiply_b(u)
+            elif op == "St":
+                store(u, js[0], COPY[rest[-1]])
+            elif op == "Ng":
+                nc.scalar.activation(out=fb_neg[:], in_=fb_sb[:], func=ACT.Copy, scale=-1.0)

@@ -24,11 +24,11 @@ N_TILES = N // P
 BANK = 512
 HALF = T // 2
 LEAD = 8
-RANGES = ((0, 256), (256, 384), (384, 512))
-XS = ((0, 256), (256, 512))
+RANGES = ((0, 384), (384, 512))
+XS = ((0, 384), (384, 512))
 PAD = BANK - RANGES[0][1]
 RUN = 4
-ORDER = "Ng0 A_00 A_01 B_00 B_01 A_023 Ca001 B_023 Cb001 Ca023 Ia0 A_1 Cb023 Ib0 B_1 Qa0 Ca1 Ia1 A_2 Qb0 Cb1 Ib1 B_2 Qa1 Ca2 Ia2 A_3 Qb1 Cb2 Ib2 B_3 St10S St11S St12S St13S Qa2 Ca3 Ia3 A_4 Qb2 Cb3 Ib3 B_4 Qa3 Ca4 Ia4 A_5 Qb3 Cb4 Ib4 B_5 Qa4 St30S St31S St32S St33S Ca5 Qb4 Ia5V Cb5 Ib5 Qa5 Qb5 St50V St51S St52V St53S"
+ORDER = "Ng0 A_00 A_01 B_00 B_01 Rb001 A_023 Ca001 Zb001 B_023 Rb023 A_101 Ca023 Zb023 Ia0 Ib0 A_123 B_101 B_123 Ca101 Cb101 Ca123 Ia1 Cb123 Ib1 Qa0 A_2 Qb0 B_2 Qa1 Ca2 Ia2 Cb2 Ib2 A_3 Qb1 Qa2 Bx3 St10S St11S St12S St13S Qb2 Da3 Qa3 Db3 Qb3 St30V St31S St32V St33S"
 
 
 def tile_mix_ahead_and_behind_kernel(tc, xf, fa, fb, wa_words, wa_scales, wb_words, wb_scales, out):
@@ -137,6 +137,28 @@ def tile_mix_ahead_and_behind_kernel(tc, xf, fa, fb, wa_words, wa_scales, wb_wor
                     out=rows_b[u][:, j, :], in0=diff[u][:, j, :], scalar1=0.0, scalar2=fb_neg[:, g, j : j + 1], op0=ALU.min, op1=ALU.mult
                 )
 
+        def subtract_peak_grouped(u):
+            diff[u] = work.tile([P, width(u), PACK], F32, name="diff")
+            nc.vector.tensor_tensor(
+                out=diff[u][:].rearrange("p (c i) j -> p c j i", i=2),
+                in0=shifted(u, every_j, 0).rearrange("p j (c i) -> p c j i", i=2),
+                in1=peak[u][:].rearrange("p j (c i) -> p c j i", i=2),
+                op=ALU.subtract,
+            )
+
+        def scale_grouped(u, factor, clip, name):
+            g = units[u][2]
+            grouped = work.tile([P, width(u), PACK], BF16, align_bytes=64, name=name)
+            nc.vector.scalar_tensor_tensor(
+                out=grouped[:],
+                in0=diff[u][:],
+                scalar=0.0,
+                in1=factor[:, g : g + 1, :].to_broadcast([P, width(u), PACK]),
+                op0=clip,
+                op1=ALU.mult,
+            )
+            return grouped
+
         def clip_b(u, js):
             if u not in short:
                 short[u] = work.tile([P, PACK, width(u)], F32, name="short")
@@ -219,6 +241,12 @@ def tile_mix_ahead_and_behind_kernel(tc, xf, fa, fb, wa_words, wa_scales, wb_wor
                 find_peak(u, sl)
             elif op == "B_":
                 subtract_peak(u, sl)
+            elif op == "Bx":
+                subtract_peak_grouped(u)
+            elif op == "Da":
+                grouped_a[u] = scale_grouped(u, fa_sb, ALU.max, "grouped_a")
+            elif op == "Db":
+                grouped_b[u] = scale_grouped(u, fb_neg, ALU.min, "grouped_b")
             elif op == "Ca":
                 scale_a(u, js)
             elif op == "Cb":

@@ -22,27 +22,34 @@ K_PASS = P * PACK
 PASSES = K // K_PASS
 N_TILES = N // P
 BANK = 512
-HALF = T // 2
+QUADRANTS = 4
+
+SPLIT = 384
+LONG, SHORT = (0, SPLIT), (SPLIT, T)
+WIDE = 256
+BACK = 2
 LEAD = 8
-RANGES = ((0, 384), (384, 512))
-XS = ((0, 384), (384, 512))
-PAD = BANK - RANGES[0][1]
-RUN = 4
-ORDER = "Ng0 A_00 A_01 B_00 B_01 Rb001 A_023 Ca001 Zb001 B_023 Rb023 A_101 Ca023 Zb023 Ia0 Ib0 A_123 B_101 B_123 Ca101 Cb101 Ca123 Ia1 Cb123 Ib1 Qa0 A_2 Qb0 B_2 Qa1 Ca2 Ia2 Cb2 Ib2 A_3 Qb1 Qa2 Bx3 St10S St11S St12S St13S Qb2 Da3 Qa3 Db3 Qb3 St30V St31S St32V St33S"
+PAD = BANK - SPLIT
+COPY_RUN = 4
+SUB_RUN = 2
 
 
 def tile_mix_ahead_and_behind_kernel(tc, xf, fa, fb, wa_words, wa_scales, wb_words, wb_scales, out):
     nc = tc.nc
-    units = [(t0, t1, g) for t0, t1 in RANGES for g in range(PASSES)]
-    last = len(units) - 1
+    pieces = [(tokens, g) for tokens in (LONG, SHORT) for g in range(PASSES)]
+    long0, long1, short0, short1 = pieces
+    all_rows, low_rows, high_rows = slice(0, PACK), slice(0, 2), slice(2, PACK)
 
     with ExitStack() as ctx:
         keep = ctx.enter_context(tc.tile_pool(name="keep", bufs=1))
-        work = ctx.enter_context(tc.tile_pool(name="work", bufs=len(units)))
+        work = ctx.enter_context(tc.tile_pool(name="work", bufs=len(pieces)))
         psum = ctx.enter_context(tc.psum_pool(name="psum", bufs=2))
         ctx.enter_context(tc.manual_schedule())
 
-        x = {(h, g): keep.tile([P, PACK, LEAD + XS[h][1] - XS[h][0]], F32, name="x%d%d" % (h, g)) for h in range(2) for g in range(PASSES)}
+        def width(piece):
+            return piece[0][1] - piece[0][0]
+
+        x = {piece: keep.tile([P, PACK, LEAD + width(piece)], F32, name="x%d" % i) for i, piece in enumerate(pieces)}
         fa_sb = keep.tile([P, PASSES, PACK], F32)
         fb_sb = keep.tile([P, PASSES, PACK], F32)
         fb_neg = keep.tile([P, PASSES, PACK], F32)
@@ -57,147 +64,138 @@ def tile_mix_ahead_and_behind_kernel(tc, xf, fa, fb, wa_words, wa_scales, wb_wor
         ub_sc = [keep.tile([P, T], U8, align_bytes=64, name="ub_sc%d" % g) for g in range(PASSES)]
 
         nc.vector.memset(zeros[:], 0.0)
-        nc.vector.memset(x[0, 0][:, :, :LEAD], 0.0)
+        nc.vector.memset(x[long0][:, :, :LEAD], 0.0)
         nc.vector.memset(wa_sc[:].bitcast(U32), 0)
         nc.vector.memset(wb_sc[:].bitcast(U32), 0)
         for g in range(PASSES):
             nc.vector.memset(ua_codes[g][:, :PAD], 0)
             nc.vector.memset(ua_sc[g][:, :PAD].bitcast(U32), 0)
 
-        def load_x(h, g, js):
-            lo = max(XS[h][0] - 2, 0)
-            hi = XS[h][1]
-            rows = xf[g * K_PASS : (g + 1) * K_PASS, lo:hi].rearrange("(p j) t -> p j t", j=PACK)
-            nc.sync.dma_start(out=x[h, g][:, js, LEAD + lo - XS[h][0] :], in_=rows[:, js, :])
+        def load_x(piece, rows):
+            (t0, t1), g = piece
+            first = max(t0 - BACK, 0)
+            source = xf[g * K_PASS : (g + 1) * K_PASS, first:t1].rearrange("(p j) t -> p j t", j=PACK)
+            nc.sync.dma_start(out=x[piece][:, rows, LEAD + first - t0 :], in_=source[:, rows, :])
 
-        def load_scales(plane, scales):
-            for q in range(4):
+        def load_scales(tile, scales):
+            for q in range(QUADRANTS):
                 nc.sync.dma_start(
-                    out=plane[32 * q : 32 * q + 4, :, :].bitcast(I32),
+                    out=tile[32 * q : 32 * q + 4, :, :].bitcast(I32),
                     in_=scales[:, 4 * q : 4 * q + 4, :].rearrange("g r c -> r g c").bitcast(I32),
                 )
 
-        every_j = slice(0, PACK)
-        j_halves = (slice(0, 2), slice(2, 4))
-        j_first = (slice(0, 1), slice(1, 2), slice(2, 4))
-        for js in j_first[:2]:
-            load_x(0, 0, js)
+        load_x(long0, slice(0, 1))
+        load_x(long0, slice(1, 2))
         nc.sync.dma_start(out=fa_sb[:], in_=fa.rearrange("(g p j) o -> p g (j o)", g=PASSES, j=PACK))
         nc.sync.dma_start(out=fb_sb[:], in_=fb.rearrange("(g p j) o -> p g (j o)", g=PASSES, j=PACK))
-        load_x(0, 0, j_first[2])
-        load_x(0, 1, every_j)
-        load_x(1, 0, every_j)
-        nc.sync.dma_start(out=wa_sb[:].bitcast(I32), in_=wa_words.rearrange("g p c -> p g c").bitcast(I32))
-        nc.sync.dma_start(out=wb_sb[:].bitcast(I32), in_=wb_words.rearrange("g p c r -> p g (c r)").bitcast(I32))
+        load_x(long0, high_rows)
+        load_x(long1, low_rows)
+        load_x(long1, high_rows)
         load_scales(wa_sc, wa_scales)
         load_scales(wb_sc, wb_scales)
-        load_x(1, 1, every_j)
+        nc.sync.dma_start(out=wa_sb[:].bitcast(I32), in_=wa_words.rearrange("g p c -> p g c").bitcast(I32))
+        load_x(short0, all_rows)
+        nc.sync.dma_start(out=wb_sb[:].bitcast(I32), in_=wb_words.rearrange("g p c r -> p g (c r)").bitcast(I32))
+        load_x(short1, all_rows)
 
-        nc.scalar.copy(out=x[0, 1][:, :, :LEAD], in_=zeros[:])
+        nc.scalar.copy(out=x[long1][:, :, :LEAD], in_=zeros[:])
 
-        short, peak, diff, rows_a, rows_b, grouped_a, grouped_b, acc = {}, {}, {}, {}, {}, {}, {}, {}
+        peak, diff, behind, rows_a, rows_b, grouped_a, grouped_b, acc = {}, {}, {}, {}, {}, {}, {}, {}
 
-        def shifted(u, js, back):
-            t0, t1, g = units[u]
-            h = 0 if t0 < XS[0][1] else 1
-            c0 = LEAD + t0 - XS[h][0] - back
-            return x[h, g][:, js, c0 : c0 + t1 - t0]
+        def piece_tile(tiles, piece, dtype, name):
+            if piece not in tiles:
+                tiles[piece] = work.tile([P, PACK, width(piece)], dtype, name=name)
+            return tiles[piece]
 
-        def pieces(w):
-            return ((0, 256), (256, 384)) if w == 384 else ((0, w),)
+        def shifted(piece, rows, back):
+            return x[piece][:, rows, LEAD - back : LEAD - back + width(piece)]
 
-        def width(u):
-            return units[u][1] - units[u][0]
+        def chunks(piece):
+            return [(c0, min(c0 + WIDE, width(piece))) for c0 in range(0, width(piece), WIDE)]
 
-        def find_peak(u, js):
-            if u not in peak:
-                peak[u] = work.tile([P, PACK, width(u)], F32, name="peak")
-            nc.vector.tensor_tensor(out=peak[u][:, js, :], in0=shifted(u, js, 1), in1=shifted(u, js, 2), op=ALU.max)
+        def find_peak(piece, rows):
+            m = piece_tile(peak, piece, F32, "peak")
+            nc.vector.tensor_tensor(out=m[:, rows, :], in0=shifted(piece, rows, 1), in1=shifted(piece, rows, 2), op=ALU.max)
 
-        def subtract_peak(u, js):
-            if u not in diff:
-                diff[u] = work.tile([P, PACK, width(u)], F32, name="diff")
-            nc.vector.tensor_tensor(out=diff[u][:, js, :], in0=shifted(u, js, 0), in1=peak[u][:, js, :], op=ALU.subtract)
+        def subtract_peak(piece, rows):
+            d = piece_tile(diff, piece, F32, "diff")
+            nc.vector.tensor_tensor(out=d[:, rows, :], in0=shifted(piece, rows, 0), in1=peak[piece][:, rows, :], op=ALU.subtract)
 
-        def scale_a(u, js):
-            g = units[u][2]
-            if u not in rows_a:
-                rows_a[u] = work.tile([P, PACK, width(u)], BF16, name="rows_a")
-            for j in js:
+        def clip_and_scale(tiles, piece, rows, clip, factor, name):
+            u = piece_tile(tiles, piece, BF16, name)
+            for j in range(rows.start, rows.stop):
                 nc.vector.tensor_scalar(
-                    out=rows_a[u][:, j, :], in0=diff[u][:, j, :], scalar1=0.0, scalar2=fa_sb[:, g, j : j + 1], op0=ALU.max, op1=ALU.mult
+                    out=u[:, j, :],
+                    in0=diff[piece][:, j, :],
+                    scalar1=0.0,
+                    scalar2=factor[:, piece[1], j : j + 1],
+                    op0=clip,
+                    op1=ALU.mult,
                 )
 
-        def scale_b(u, js):
-            g = units[u][2]
-            if u not in rows_b:
-                rows_b[u] = work.tile([P, PACK, width(u)], BF16, name="rows_b")
-            for j in js:
-                nc.vector.tensor_scalar(
-                    out=rows_b[u][:, j, :], in0=diff[u][:, j, :], scalar1=0.0, scalar2=fb_neg[:, g, j : j + 1], op0=ALU.min, op1=ALU.mult
+        def make_ua(piece, rows):
+            clip_and_scale(rows_a, piece, rows, ALU.max, fa_sb, "rows_a")
+
+        def make_ub(piece, rows):
+            clip_and_scale(rows_b, piece, rows, ALU.min, fb_neg, "rows_b")
+
+        def clip_behind_on_scalar(piece, rows):
+            b = piece_tile(behind, piece, F32, "behind")
+            nc.scalar.activation(out=b[:, rows, :], in_=diff[piece][:, rows, :], func=ACT.Relu, scale=-1.0)
+
+        def scale_behind_on_scalar(piece, rows):
+            u = piece_tile(rows_b, piece, BF16, "rows_b")
+            for j in range(rows.start, rows.stop):
+                nc.scalar.activation(
+                    out=u[:, j, :], in_=behind[piece][:, j, :], func=ACT.Copy, scale=fb_sb[:, piece[1], j : j + 1]
                 )
 
-        def subtract_peak_grouped(u):
-            diff[u] = work.tile([P, width(u), PACK], F32, name="diff")
+        def regroup(copy, rows_tile, name):
+            grouped = work.tile([P, rows_tile.shape[2], PACK], BF16, align_bytes=64, name=name)
+            copy(
+                out=grouped[:].rearrange("p (c i) j -> p c j i", i=COPY_RUN),
+                in_=rows_tile[:].rearrange("p j (c i) -> p c j i", i=COPY_RUN),
+            )
+            return grouped
+
+        def regroup_ua(piece, copy):
+            grouped_a[piece] = regroup(copy, rows_a[piece], "grouped_a")
+
+        def regroup_ub(piece, copy):
+            grouped_b[piece] = regroup(copy, rows_b[piece], "grouped_b")
+
+        def subtract_peak_grouped(piece):
+            diff[piece] = work.tile([P, width(piece), PACK], F32, name="diff")
             nc.vector.tensor_tensor(
-                out=diff[u][:].rearrange("p (c i) j -> p c j i", i=2),
-                in0=shifted(u, every_j, 0).rearrange("p j (c i) -> p c j i", i=2),
-                in1=peak[u][:].rearrange("p j (c i) -> p c j i", i=2),
+                out=diff[piece][:].rearrange("p (c i) j -> p c j i", i=SUB_RUN),
+                in0=shifted(piece, all_rows, 0).rearrange("p j (c i) -> p c j i", i=SUB_RUN),
+                in1=peak[piece][:].rearrange("p j (c i) -> p c j i", i=SUB_RUN),
                 op=ALU.subtract,
             )
 
-        def scale_grouped(u, factor, clip, name):
-            g = units[u][2]
-            grouped = work.tile([P, width(u), PACK], BF16, align_bytes=64, name=name)
+        def clip_and_scale_grouped(piece, clip, factor, name):
+            g = piece[1]
+            grouped = work.tile([P, width(piece), PACK], BF16, align_bytes=64, name=name)
             nc.vector.scalar_tensor_tensor(
                 out=grouped[:],
-                in0=diff[u][:],
+                in0=diff[piece][:],
                 scalar=0.0,
-                in1=factor[:, g : g + 1, :].to_broadcast([P, width(u), PACK]),
+                in1=factor[:, g : g + 1, :].to_broadcast([P, width(piece), PACK]),
                 op0=clip,
                 op1=ALU.mult,
             )
             return grouped
 
-        def clip_b(u, js):
-            if u not in short:
-                short[u] = work.tile([P, PACK, width(u)], F32, name="short")
-            nc.scalar.activation(out=short[u][:, js, :], in_=diff[u][:, js, :], func=ACT.Relu, scale=-1.0)
-
-        def scale_b_scalar(u, js):
-            g = units[u][2]
-            if u not in rows_b:
-                rows_b[u] = work.tile([P, PACK, width(u)], BF16, name="rows_b")
-            for j in js:
-                nc.scalar.activation(out=rows_b[u][:, j, :], in_=short[u][:, j, :], func=ACT.Copy, scale=fb_sb[:, g, j : j + 1])
-
-        def interleave(copy, rows, name):
-            grouped = work.tile([P, rows.shape[2], PACK], BF16, align_bytes=64, name=name)
-            copy(
-                out=grouped[:].rearrange("p (c i) j -> p c j i", i=RUN),
-                in_=rows[:].rearrange("p j (c i) -> p c j i", i=RUN),
-            )
-            return grouped
-
-        def quantize_a(u):
-            t0, t1, g = units[u]
-            for c0, c1 in pieces(t1 - t0):
+        def product_a(piece):
+            (t0, t1), g = piece
+            for c0, c1 in chunks(piece):
                 cols = slice(PAD + t0 + c0, PAD + t0 + c1)
                 nc.vector.quantize_mx(
-                    out=ua_codes[g][:, cols].bitcast(E5M2X4), scales=ua_sc[g][:, cols], in_=grouped_a[u][:, c0:c1, :].rearrange("p t j -> p (t j)")
+                    out=ua_codes[g][:, cols].bitcast(E5M2X4),
+                    scales=ua_sc[g][:, cols],
+                    in_=grouped_a[piece][:, c0:c1, :].rearrange("p t j -> p (t j)"),
                 )
-
-        def quantize_b(u):
-            t0, t1, g = units[u]
-            for c0, c1 in pieces(t1 - t0):
-                cols = slice(t0 + c0, t0 + c1)
-                nc.vector.quantize_mx(
-                    out=ub_codes[g][:, cols].bitcast(E4M3X4), scales=ub_sc[g][:, cols], in_=grouped_b[u][:, c0:c1, :].rearrange("p t j -> p (t j)")
-                )
-
-        def multiply_a(u):
-            t0, t1, g = units[u]
-            cols = slice(PAD + t1 - BANK, PAD + t1)
+            window = slice(PAD + t1 - BANK, PAD + t1)
             for n in range(N_TILES):
                 if g == 0:
                     acc[t0, n] = psum.tile([P, BANK], F32, name="acc%d" % n)
@@ -205,67 +203,87 @@ def tile_mix_ahead_and_behind_kernel(tc, xf, fa, fb, wa_words, wa_scales, wb_wor
                     out=acc[t0, n][:],
                     lhsT=wa_sb[:, g, 2 * P * n : 2 * P * (n + 1)].bitcast(E2M1X4),
                     lhsT_scale=wa_sc[:, g, P * n : P * (n + 1)],
-                    rhs=ua_codes[g][:, cols].bitcast(E5M2X4),
-                    rhs_scale=ua_sc[g][:, cols],
+                    rhs=ua_codes[g][:, window].bitcast(E5M2X4),
+                    rhs_scale=ua_sc[g][:, window],
                     start=(g == 0),
                     stop=False,
                 )
 
-        def multiply_b(u):
-            t0, t1, g = units[u]
+        def product_b(piece):
+            (t0, t1), g = piece
+            for c0, c1 in chunks(piece):
+                nc.vector.quantize_mx(
+                    out=ub_codes[g][:, t0 + c0 : t0 + c1].bitcast(E4M3X4),
+                    scales=ub_sc[g][:, t0 + c0 : t0 + c1],
+                    in_=grouped_b[piece][:, c0:c1, :].rearrange("p t j -> p (t j)"),
+                )
+            first_col = BANK - width(piece)
             for n in range(N_TILES):
-                for c0, c1 in pieces(t1 - t0):
+                for c0, c1 in chunks(piece):
                     nc.tensor.matmul_mx(
-                        out=acc[t0, n][:, BANK - (t1 - t0) + c0 : BANK - (t1 - t0) + c1],
+                        out=acc[t0, n][:, first_col + c0 : first_col + c1],
                         lhsT=wb_sb[:, g, P * n : P * (n + 1)].bitcast(E4M3X4),
                         lhsT_scale=wb_sc[:, g, P * n : P * (n + 1)],
                         rhs=ub_codes[g][:, t0 + c0 : t0 + c1].bitcast(E4M3X4),
                         rhs_scale=ub_sc[g][:, t0 + c0 : t0 + c1],
                         start=False,
-                        stop=(g == PASSES - 1 and c1 == t1 - t0),
+                        stop=(g == PASSES - 1 and t0 + c1 == t1),
                     )
 
-        def store(u, n, copy):
-            t0, t1, g = units[u]
+        def store(tokens, n, copy):
+            t0, t1 = tokens
             result = work.tile([P, t1 - t0], F32, name="result%d" % n)
             copy(out=result[:], in_=acc[t0, n][:, BANK - (t1 - t0) :])
             nc.sync.dma_start(out=out[P * n : P * (n + 1), t0:t1], in_=result[:])
 
-        COPY = {"S": nc.scalar.copy, "V": nc.vector.tensor_copy}
-        for tok in ORDER.split():
-            op, u = tok[:2], int(tok[2])
-            rest = tok[3:]
-            js = [int(c) for c in rest if c in "0123"] or [0, 1, 2, 3]
-            sl = slice(js[0], js[-1] + 1)
-            if op == "A_":
-                find_peak(u, sl)
-            elif op == "B_":
-                subtract_peak(u, sl)
-            elif op == "Bx":
-                subtract_peak_grouped(u)
-            elif op == "Da":
-                grouped_a[u] = scale_grouped(u, fa_sb, ALU.max, "grouped_a")
-            elif op == "Db":
-                grouped_b[u] = scale_grouped(u, fb_neg, ALU.min, "grouped_b")
-            elif op == "Ca":
-                scale_a(u, js)
-            elif op == "Cb":
-                scale_b(u, js)
-            elif op == "Rb":
-                clip_b(u, sl)
-            elif op == "Zb":
-                scale_b_scalar(u, js)
-            elif op == "Ia":
-                grouped_a[u] = interleave(COPY[rest or "S"], rows_a[u], "grouped_a")
-            elif op == "Ib":
-                grouped_b[u] = interleave(COPY[rest or "S"], rows_b[u], "grouped_b")
-            elif op == "Qa":
-                quantize_a(u)
-                multiply_a(u)
-            elif op == "Qb":
-                quantize_b(u)
-                multiply_b(u)
-            elif op == "St":
-                store(u, js[0], COPY[rest[-1]])
-            elif op == "Ng":
-                nc.scalar.activation(out=fb_neg[:], in_=fb_sb[:], func=ACT.Copy, scale=-1.0)
+        nc.scalar.activation(out=fb_neg[:], in_=fb_sb[:], func=ACT.Copy, scale=-1.0)
+
+
+        for j in (0, 1):
+            find_peak(long0, slice(j, j + 1))
+        for j in (0, 1):
+            subtract_peak(long0, slice(j, j + 1))
+        clip_behind_on_scalar(long0, low_rows)
+        find_peak(long0, high_rows)
+        make_ua(long0, low_rows)
+        scale_behind_on_scalar(long0, low_rows)
+        subtract_peak(long0, high_rows)
+        clip_behind_on_scalar(long0, high_rows)
+        find_peak(long1, low_rows)
+        make_ua(long0, high_rows)
+        scale_behind_on_scalar(long0, high_rows)
+        regroup_ua(long0, nc.scalar.copy)
+        regroup_ub(long0, nc.scalar.copy)
+
+        find_peak(long1, high_rows)
+        subtract_peak(long1, low_rows)
+        subtract_peak(long1, high_rows)
+        find_peak(short0, all_rows)
+        product_a(long0)
+        make_ua(long1, all_rows)
+        regroup_ua(long1, nc.scalar.copy)
+        subtract_peak(short0, all_rows)
+        product_b(long0)
+        make_ub(long1, all_rows)
+        regroup_ub(long1, nc.scalar.copy)
+
+        make_ua(short0, all_rows)
+        product_a(long1)
+        regroup_ua(short0, nc.vector.tensor_copy)
+        find_peak(short1, all_rows)
+        product_a(short0)
+        make_ub(short0, all_rows)
+        regroup_ub(short0, nc.scalar.copy)
+        product_b(long1)
+
+        subtract_peak_grouped(short1)
+        for n in range(N_TILES):
+            store(LONG, n, nc.scalar.copy)
+        product_b(short0)
+        grouped_a[short1] = clip_and_scale_grouped(short1, ALU.max, fa_sb, "grouped_a")
+        product_a(short1)
+        grouped_b[short1] = clip_and_scale_grouped(short1, ALU.min, fb_neg, "grouped_b")
+        product_b(short1)
+
+        for n in range(N_TILES):
+            store(SHORT, n, nc.vector.tensor_copy if n % 2 == 0 else nc.scalar.copy)

from contextlib import ExitStack

import concourse.mybir as mybir

K, T, N = 1024, 512, 512
FLOPS = 2 * 2 * K * T * N

F32 = mybir.dt.float32
BF16 = mybir.dt.bfloat16
I32 = mybir.dt.int32
U32 = mybir.dt.uint32
U8 = mybir.dt.uint8
E2M1X4 = mybir.dt.float4_e2m1fn_x4
E4M3X4 = mybir.dt.float8_e4m3fn_x4
E5M2X4 = mybir.dt.float8_e5m2_x4
ALU = mybir.AluOpType
ACT = mybir.ActivationFunctionType

P = 128
PACK = 4
K_PASS = P * PACK
PASSES = K // K_PASS
N_TILES = N // P
BANK = 512
QUADRANTS = 4

SPLIT = 384
LONG, SHORT = (0, SPLIT), (SPLIT, T)
WIDE = 256
BACK = 2
LEAD = 8
PAD = BANK - SPLIT
COPY_RUN = 4
SUB_RUN = 2


def tile_mix_ahead_and_behind_kernel(tc, xf, fa, fb, wa_words, wa_scales, wb_words, wb_scales, out):
    nc = tc.nc
    pieces = [(tokens, g) for tokens in (LONG, SHORT) for g in range(PASSES)]
    long0, long1, short0, short1 = pieces
    all_rows, low_rows, high_rows = slice(0, PACK), slice(0, 2), slice(2, PACK)

    with ExitStack() as ctx:
        keep = ctx.enter_context(tc.tile_pool(name="keep", bufs=1))
        work = ctx.enter_context(tc.tile_pool(name="work", bufs=len(pieces)))
        psum = ctx.enter_context(tc.psum_pool(name="psum", bufs=2))
        ctx.enter_context(tc.manual_schedule())

        def width(piece):
            return piece[0][1] - piece[0][0]

        x = {piece: keep.tile([P, PACK, LEAD + width(piece)], F32, name="x%d" % i) for i, piece in enumerate(pieces)}
        fa_sb = keep.tile([P, PASSES, PACK], F32)
        fb_sb = keep.tile([P, PASSES, PACK], F32)
        fb_neg = keep.tile([P, PASSES, PACK], F32)
        zeros = keep.tile([P, PACK, LEAD], F32)
        wa_sb = keep.tile([P, PASSES, 2 * N], U8, align_bytes=64)
        wb_sb = keep.tile([P, PASSES, N], U32, align_bytes=64)
        wa_sc = keep.tile([P, PASSES, N], U8, align_bytes=64)
        wb_sc = keep.tile([P, PASSES, N], U8, align_bytes=64)
        ua_codes = [keep.tile([P, PAD + T], U32, align_bytes=64, name="ua_codes%d" % g) for g in range(PASSES)]
        ua_sc = [keep.tile([P, PAD + T], U8, align_bytes=64, name="ua_sc%d" % g) for g in range(PASSES)]
        ub_codes = [keep.tile([P, T], U32, align_bytes=64, name="ub_codes%d" % g) for g in range(PASSES)]
        ub_sc = [keep.tile([P, T], U8, align_bytes=64, name="ub_sc%d" % g) for g in range(PASSES)]

        nc.vector.memset(zeros[:], 0.0)
        nc.vector.memset(x[long0][:, :, :LEAD], 0.0)
        nc.vector.memset(wa_sc[:].bitcast(U32), 0)
        nc.vector.memset(wb_sc[:].bitcast(U32), 0)
        for g in range(PASSES):
            nc.vector.memset(ua_codes[g][:, :PAD], 0)
            nc.vector.memset(ua_sc[g][:, :PAD].bitcast(U32), 0)

        def load_x(piece, rows):
            (t0, t1), g = piece
            first = max(t0 - BACK, 0)
            source = xf[g * K_PASS : (g + 1) * K_PASS, first:t1].rearrange("(p j) t -> p j t", j=PACK)
            nc.sync.dma_start(out=x[piece][:, rows, LEAD + first - t0 :], in_=source[:, rows, :])

        def load_scales(tile, scales):
            for q in range(QUADRANTS):
                nc.sync.dma_start(
                    out=tile[32 * q : 32 * q + 4, :, :].bitcast(I32),
                    in_=scales[:, 4 * q : 4 * q + 4, :].rearrange("g r c -> r g c").bitcast(I32),
                )

        load_x(long0, slice(0, 1))
        load_x(long0, slice(1, 2))
        nc.sync.dma_start(out=fa_sb[:], in_=fa.rearrange("(g p j) o -> p g (j o)", g=PASSES, j=PACK))
        nc.sync.dma_start(out=fb_sb[:], in_=fb.rearrange("(g p j) o -> p g (j o)", g=PASSES, j=PACK))
        load_x(long0, high_rows)
        load_x(long1, low_rows)
        load_x(long1, high_rows)
        load_scales(wa_sc, wa_scales)
        load_scales(wb_sc, wb_scales)
        nc.sync.dma_start(out=wa_sb[:].bitcast(I32), in_=wa_words.rearrange("g p c -> p g c").bitcast(I32))
        load_x(short0, all_rows)
        nc.sync.dma_start(out=wb_sb[:].bitcast(I32), in_=wb_words.rearrange("g p c r -> p g (c r)").bitcast(I32))
        load_x(short1, all_rows)

        nc.scalar.copy(out=x[long1][:, :, :LEAD], in_=zeros[:])

        peak, diff, behind, rows_a, rows_b, grouped_a, grouped_b, acc = {}, {}, {}, {}, {}, {}, {}, {}

        def piece_tile(tiles, piece, dtype, name):
            if piece not in tiles:
                tiles[piece] = work.tile([P, PACK, width(piece)], dtype, name=name)
            return tiles[piece]

        def shifted(piece, rows, back):
            return x[piece][:, rows, LEAD - back : LEAD - back + width(piece)]

        def chunks(piece):
            return [(c0, min(c0 + WIDE, width(piece))) for c0 in range(0, width(piece), WIDE)]

        def find_peak(piece, rows):
            m = piece_tile(peak, piece, F32, "peak")
            nc.vector.tensor_tensor(out=m[:, rows, :], in0=shifted(piece, rows, 1), in1=shifted(piece, rows, 2), op=ALU.max)

        def subtract_peak(piece, rows):
            d = piece_tile(diff, piece, F32, "diff")
            nc.vector.tensor_tensor(out=d[:, rows, :], in0=shifted(piece, rows, 0), in1=peak[piece][:, rows, :], op=ALU.subtract)

        def clip_and_scale(tiles, piece, rows, clip, factor, name):
            u = piece_tile(tiles, piece, BF16, name)
            for j in range(rows.start, rows.stop):
                nc.vector.tensor_scalar(
                    out=u[:, j, :],
                    in0=diff[piece][:, j, :],
                    scalar1=0.0,
                    scalar2=factor[:, piece[1], j : j + 1],
                    op0=clip,
                    op1=ALU.mult,
                )

        def make_ua(piece, rows):
            clip_and_scale(rows_a, piece, rows, ALU.max, fa_sb, "rows_a")

        def make_ub(piece, rows):
            clip_and_scale(rows_b, piece, rows, ALU.min, fb_neg, "rows_b")

        def clip_behind_on_scalar(piece, rows):
            b = piece_tile(behind, piece, F32, "behind")
            nc.scalar.activation(out=b[:, rows, :], in_=diff[piece][:, rows, :], func=ACT.Relu, scale=-1.0)

        def scale_behind_on_scalar(piece, rows):
            u = piece_tile(rows_b, piece, BF16, "rows_b")
            for j in range(rows.start, rows.stop):
                nc.scalar.activation(
                    out=u[:, j, :], in_=behind[piece][:, j, :], func=ACT.Copy, scale=fb_sb[:, piece[1], j : j + 1]
                )

        def regroup(copy, rows_tile, name):
            grouped = work.tile([P, rows_tile.shape[2], PACK], BF16, align_bytes=64, name=name)
            copy(
                out=grouped[:].rearrange("p (c i) j -> p c j i", i=COPY_RUN),
                in_=rows_tile[:].rearrange("p j (c i) -> p c j i", i=COPY_RUN),
            )
            return grouped

        def regroup_ua(piece, copy):
            grouped_a[piece] = regroup(copy, rows_a[piece], "grouped_a")

        def regroup_ub(piece, copy):
            grouped_b[piece] = regroup(copy, rows_b[piece], "grouped_b")

        def subtract_peak_grouped(piece):
            diff[piece] = work.tile([P, width(piece), PACK], F32, name="diff")
            nc.vector.tensor_tensor(
                out=diff[piece][:].rearrange("p (c i) j -> p c j i", i=SUB_RUN),
                in0=shifted(piece, all_rows, 0).rearrange("p j (c i) -> p c j i", i=SUB_RUN),
                in1=peak[piece][:].rearrange("p j (c i) -> p c j i", i=SUB_RUN),
                op=ALU.subtract,
            )

        def clip_and_scale_grouped(piece, clip, factor, name):
            g = piece[1]
            grouped = work.tile([P, width(piece), PACK], BF16, align_bytes=64, name=name)
            nc.vector.scalar_tensor_tensor(
                out=grouped[:],
                in0=diff[piece][:],
                scalar=0.0,
                in1=factor[:, g : g + 1, :].to_broadcast([P, width(piece), PACK]),
                op0=clip,
                op1=ALU.mult,
            )
            return grouped

        def product_a(piece):
            (t0, t1), g = piece
            for c0, c1 in chunks(piece):
                cols = slice(PAD + t0 + c0, PAD + t0 + c1)
                nc.vector.quantize_mx(
                    out=ua_codes[g][:, cols].bitcast(E5M2X4),
                    scales=ua_sc[g][:, cols],
                    in_=grouped_a[piece][:, c0:c1, :].rearrange("p t j -> p (t j)"),
                )
            window = slice(PAD + t1 - BANK, PAD + t1)
            for n in range(N_TILES):
                if g == 0:
                    acc[t0, n] = psum.tile([P, BANK], F32, name="acc%d" % n)
                nc.tensor.matmul_mx(
                    out=acc[t0, n][:],
                    lhsT=wa_sb[:, g, 2 * P * n : 2 * P * (n + 1)].bitcast(E2M1X4),
                    lhsT_scale=wa_sc[:, g, P * n : P * (n + 1)],
                    rhs=ua_codes[g][:, window].bitcast(E5M2X4),
                    rhs_scale=ua_sc[g][:, window],
                    start=(g == 0),
                    stop=False,
                )

        def product_b(piece):
            (t0, t1), g = piece
            for c0, c1 in chunks(piece):
                nc.vector.quantize_mx(
                    out=ub_codes[g][:, t0 + c0 : t0 + c1].bitcast(E4M3X4),
                    scales=ub_sc[g][:, t0 + c0 : t0 + c1],
                    in_=grouped_b[piece][:, c0:c1, :].rearrange("p t j -> p (t j)"),
                )
            first_col = BANK - width(piece)
            for n in range(N_TILES):
                for c0, c1 in chunks(piece):
                    nc.tensor.matmul_mx(
                        out=acc[t0, n][:, first_col + c0 : first_col + c1],
                        lhsT=wb_sb[:, g, P * n : P * (n + 1)].bitcast(E4M3X4),
                        lhsT_scale=wb_sc[:, g, P * n : P * (n + 1)],
                        rhs=ub_codes[g][:, t0 + c0 : t0 + c1].bitcast(E4M3X4),
                        rhs_scale=ub_sc[g][:, t0 + c0 : t0 + c1],
                        start=False,
                        stop=(g == PASSES - 1 and t0 + c1 == t1),
                    )

        def store(tokens, n, copy):
            t0, t1 = tokens
            result = work.tile([P, t1 - t0], F32, name="result%d" % n)
            copy(out=result[:], in_=acc[t0, n][:, BANK - (t1 - t0) :])
            nc.sync.dma_start(out=out[P * n : P * (n + 1), t0:t1], in_=result[:])

        nc.scalar.activation(out=fb_neg[:], in_=fb_sb[:], func=ACT.Copy, scale=-1.0)


        for j in (0, 1):
            find_peak(long0, slice(j, j + 1))
        for j in (0, 1):
            subtract_peak(long0, slice(j, j + 1))
        clip_behind_on_scalar(long0, low_rows)
        find_peak(long0, high_rows)
        make_ua(long0, low_rows)
        scale_behind_on_scalar(long0, low_rows)
        subtract_peak(long0, high_rows)
        clip_behind_on_scalar(long0, high_rows)
        find_peak(long1, low_rows)
        make_ua(long0, high_rows)
        scale_behind_on_scalar(long0, high_rows)
        regroup_ua(long0, nc.scalar.copy)
        regroup_ub(long0, nc.scalar.copy)

        find_peak(long1, high_rows)
        subtract_peak(long1, low_rows)
        subtract_peak(long1, high_rows)
        find_peak(short0, all_rows)
        product_a(long0)
        make_ua(long1, all_rows)
        regroup_ua(long1, nc.scalar.copy)
        subtract_peak(short0, all_rows)
        product_b(long0)
        make_ub(long1, all_rows)
        regroup_ub(long1, nc.scalar.copy)

        make_ua(short0, all_rows)
        product_a(long1)
        regroup_ua(short0, nc.vector.tensor_copy)
        find_peak(short1, all_rows)
        product_a(short0)
        make_ub(short0, all_rows)
        regroup_ub(short0, nc.scalar.copy)
        product_b(long1)

        subtract_peak_grouped(short1)
        for n in range(N_TILES):
            store(LONG, n, nc.scalar.copy)
        product_b(short0)
        grouped_a[short1] = clip_and_scale_grouped(short1, ALU.max, fa_sb, "grouped_a")
        product_a(short1)
        grouped_b[short1] = clip_and_scale_grouped(short1, ALU.min, fb_neg, "grouped_b")
        product_b(short1)

        for n in range(N_TILES):
            store(SHORT, n, nc.vector.tensor_copy if n % 2 == 0 else nc.scalar.copy)
